import numpy as np
import ml_dtypes


def mxq(x, axis, fmt="e4m3"):
    dtype, down = {"e4m3": (ml_dtypes.float8_e4m3fn, 7), "e5m2": (ml_dtypes.float8_e5m2, 14)}[fmt]
    v = np.moveaxis(np.asarray(x, np.float32).astype(ml_dtypes.bfloat16).astype(np.float64), axis, -1)
    blocks = v.reshape(v.shape[:-1] + (-1, 32))
    amax = np.abs(blocks).max(-1, keepdims=True)
    byte = np.maximum(np.where(amax > 0, np.frexp(amax)[1] - 1 + 127, 0) - down, 1)
    scale = np.exp2(byte - 127.0)
    codes = (blocks / scale).astype(np.float32).astype(dtype).astype(np.float64)
    return np.moveaxis((codes * scale).reshape(v.shape), -1, axis)


WIDE = False


def mx_kscale(k):
    if not WIDE:
        return np.ones(k)
    levels = np.array([10, -10, 5, -5, 0])
    if k % 512:
        return np.exp2(np.random.permutation(np.resize(levels, k // 32))).repeat(32)
    a = np.empty((k // 512, 16))
    for p in range(k // 512):
        a[p, :8] = np.random.permutation(np.resize(levels, 8))
        for g in range(8):
            far = levels[np.abs(levels - a[p, g]) >= 10]
            a[p, g + 8] = far[np.random.randint(len(far))]
    return np.exp2(a.ravel()).repeat(32)


def f64(x):
    return np.asarray(x).astype(np.float64)


def striped(idx):
    return np.tile(idx.reshape(-1, 16).T, (8, 1)).astype(np.uint16)


def unstriped(offs):
    return offs[:16].T.reshape(-1).astype(np.int64)


def striped8(idx):
    return np.concatenate([x.reshape(-1, 16).T for x in idx]).astype(np.uint16)


def runs(offs, k):
    lists = np.stack([offs[16 * r : 16 * r + 16].T.reshape(-1) for r in range(8)]).astype(np.int64)
    return lists[np.arange(k) % 512 // 64]


def pack_weight(w):
    k, n = w.shape
    w = f64(np.asarray(w, np.float32).astype(ml_dtypes.bfloat16)).reshape(k // 32, 32, n)
    amax = np.abs(w).max(1)
    byte = np.clip(np.where(amax > 0, np.frexp(amax)[1] - 1 + 127 - 7, 1), 1, 254)
    scaled = (w * np.exp2(127.0 - byte)[:, None, :]).reshape(k, n).astype(np.float32)
    words = np.ascontiguousarray(scaled.reshape(k // 512, 128, 4, n).transpose(0, 1, 3, 2)).astype(ml_dtypes.float8_e4m3fn).view(np.uint8)
    return words, np.ascontiguousarray(byte.astype(np.uint8).reshape(k // 512, 16, n))


def unpack_weight(words, scales):
    g, p, n, _ = words.shape
    vals = np.ascontiguousarray(words).view(ml_dtypes.float8_e4m3fn).astype(np.float64) * np.repeat(np.exp2(scales.astype(np.float64) - 127.0), 8, axis=1)[..., None]
    return vals.transpose(0, 1, 3, 2).reshape(g * 512, n)


def sigmoid(v):
    return 1.0 / (1.0 + np.exp(-np.maximum(v, -700.0)))


K, T, S, H, W, C = 512, 2048, 512, 512, 2048, 512


def setup_inputs():
    n = np.random.standard_normal
    s = mx_kscale(K)[:, None]
    packed_xT = pack_weight(n((K, T)) * s)
    return {
        "x_words": packed_xT[0],
        "x_scales": packed_xT[1],
        "w1": (n((K, H)) / np.sqrt(K) / s).astype(np.float32),
        "sl": np.random.uniform(1.5, 3.0, (H, 1)).astype(np.float32),
        "th": (0.5 * n((H, 1))).astype(np.float32),
        "gs": (np.random.uniform(0.5, 1.5, (K, 1)) / s).astype(np.float32),
        "sl2": np.random.uniform(1.0, 2.0, (C, 1)).astype(np.float32),
        "th2": (0.5 * n((C, 1))).astype(np.float32),
        "offs": striped(np.random.permutation(T)[:S]),
        "n1": striped(np.random.randint(0, S, W)),
        "ca": striped(np.random.permutation(T)[:C]),
        "cb": striped(np.random.permutation(T)[:C]),
        "cd": striped(np.random.permutation(T)[:C]),
        "n2": striped8(np.stack([np.random.permutation(S) for _ in range(8)])),
        "n3": striped8(np.stack([np.random.permutation(S) for _ in range(8)])),
        "n4": striped(np.random.permutation(S)),
        "n5": striped(np.random.permutation(S)),
    }


def reference(x_words, x_scales, w1, sl, th, gs, sl2, th2, offs, n1, ca, cb, cd, n2, n3, n4, n5):
    x_ca = unpack_weight(x_words, x_scales)[:, unstriped(ca)]
    xq = unpack_weight(x_words, x_scales)[:, unstriped(offs)]
    y = mxq(f64(w1), 0, "e4m3").T @ xq
    sg = sigmoid(f64(sl) * (y[:, unstriped(n1)] - f64(th)))
    cnt = sg.reshape(H, S, 4).sum(axis=2)
    z = f64(gs) * np.maximum(y, cnt + -1.5)
    zq = mxq(z, 0, "e4m3")
    a = 0.0625 * (x_ca.T @ zq)
    x_cb = unpack_weight(x_words, x_scales)[:, unstriped(cb)]
    b = 0.0625 * (x_cb.T @ zq)
    sg2 = sigmoid(f64(sl2) * (b[np.arange(C)[:, None], runs(n2, C)] - f64(th2)))
    m1 = a * sg2 - (0.5 * (a[np.arange(C)[:, None], runs(n3, C)]))
    x_cd = unpack_weight(x_words, x_scales)[:, unstriped(cd)]
    q = 0.0625 * (x_cd.T @ zq)
    return np.maximum(m1, q[:, unstriped(n5)]) - (np.minimum(m1[:, unstriped(n4)], q))

@@ -1,0 +1,286 @@
+from contextlib import ExitStack
+
+import concourse.mybir as mybir
+
+F32 = mybir.dt.float32
+BF16 = mybir.dt.bfloat16
+I32 = mybir.dt.int32
+U32 = mybir.dt.uint32
+U16 = mybir.dt.uint16
+U8 = mybir.dt.uint8
+FP8X4 = mybir.dt.float8_e4m3fn_x4
+ALU = mybir.AluOpType
+ACT = mybir.ActivationFunctionType
+
+P = 128
+PACK = 4
+T = 2048
+S = 512
+MEMBERS = 4
+PIECE = 256
+CHUNKS = (256, 128, 128)
+FLOPS = 4 * 2 * 512 * 512 * 512
+
+
+def tile_picked_tricdgxbmaxbegc_none_p_kernel(
+    tc, x_words, x_scales, w1, sl, th, gs, sl2, th2, offs, n1, ca, cb, cd, n2, n3, n4, n5, out
+):
+    nc = tc.nc
+    with ExitStack() as ctx:
+        keep = ctx.enter_context(tc.tile_pool(name="keep", bufs=1))
+        psum = ctx.enter_context(tc.psum_pool(name="psum", bufs=8))
+
+        def load_list(src, name):
+            dst = keep.tile([P, src.shape[1]], U16, name=name)
+            nc.sync.dma_start(dst[:], src)
+            return dst
+
+        def load_column(src, name, queue):
+            dst = keep.tile([P, PACK], F32, name=name)
+            queue.dma_start(dst[:], src.rearrange("(p t) o -> p (t o)", t=PACK))
+            return dst
+
+        def piece(lst, first):
+            return lst[:, first // 16 : (first + PIECE) // 16]
+
+        table_scales = keep.tile([P, T], U8, name="table_scales", align_bytes=64)
+        nc.vector.memset(table_scales[:].bitcast(I32), 0)
+        w_rows = w1.rearrange("(p j) c -> p j c", j=PACK)
+        w_half = [keep.tile([P, PACK, S // 2], F32, name=f"w_half{h}") for h in range(2)]
+        nc.sync.dma_start(w_half[0][:], w_rows[:, :, : S // 2])
+        for quad in range(4):
+            nc.sync.dma_start(
+                table_scales[32 * quad : 32 * quad + 4, :].bitcast(I32),
+                x_scales[0, 4 * quad : 4 * quad + 4, :].bitcast(I32),
+            )
+        offs_l = load_list(offs, "offs_l")
+        nc.sync.dma_start(w_half[1][:], w_rows[:, :, S // 2 :])
+        cb_l = load_list(cb, "cb_l")
+        table_words = keep.tile([P, T], U32, name="table_words", align_bytes=64)
+        nc.sync.dma_start(
+            table_words[:].bitcast(I32), x_words[0].rearrange("p n t -> p (n t)").bitcast(I32)
+        )
+        slope = load_column(sl, "slope", nc.gpsimd)
+        thresh = load_column(th, "thresh", nc.gpsimd)
+        n1_l = load_list(n1, "n1_l")
+        gain = load_column(gs, "gain", nc.sync)
+        ca_l = load_list(ca, "ca_l")
+        cd_l = load_list(cd, "cd_l")
+        slope2 = load_column(sl2, "slope2", nc.sync)
+        thresh2 = load_column(th2, "thresh2", nc.sync)
+        n2_l = load_list(n2, "n2_l")
+        n3_l = load_list(n3, "n3_l")
+        n5_l = load_list(n5, "n5_l")
+        n4_l = load_list(n4, "n4_l")
+
+        def pick(table, lst, dtype, name, dealt):
+            dst = keep.tile([P, S], dtype, name=name, align_bytes=64)
+            view = dst[:].rearrange("p (t m) -> p m t", t=PACK) if dealt else dst[:]
+            nc.vector.tensor_copy(view, table[:].indirect(lst[:]))
+            return dst
+
+        w_bf = keep.tile([P, PACK * S], BF16, name="w_bf", align_bytes=64)
+        w_bf_view = w_bf[:].rearrange("p (t m j) -> p m t j", t=PACK, j=PACK)
+        for h in range(2):
+            nc.scalar.copy(
+                w_bf_view[:, h * (P // 2) : (h + 1) * (P // 2)],
+                w_half[h][:].rearrange("p j (m t) -> p m t j", t=PACK),
+            )
+        xq_scales = pick(table_scales, offs_l, U8, "xq_scales", False)
+        xb_scales = pick(table_scales, cb_l, U8, "xb_scales", True)
+        w_words = keep.tile([P, S], U32, name="w_words", align_bytes=64)
+        w_scales = keep.tile([P, S], U8, name="w_scales", align_bytes=64)
+        nc.vector.quantize_mx(w_words[:].bitcast(FP8X4), w_scales[:], w_bf[:])
+        xq_words = pick(table_words, offs_l, U32, "xq_words", False)
+        bias = keep.tile([P, PACK], F32, name="bias")
+        nc.vector.scalar_tensor_tensor(bias[:], slope[:], -1.0, thresh[:], ALU.mult, ALU.mult)
+
+        def product(bank, words, scales, t, rhs_words, rhs_scales, cols):
+            rows = slice(t * P, (t + 1) * P)
+            nc.tensor.matmul_mx(
+                bank[:, cols],
+                lhsT=words[:, rows].bitcast(FP8X4),
+                lhsT_scale=scales[:, rows],
+                rhs=rhs_words[:, cols].bitcast(FP8X4),
+                rhs_scale=rhs_scales[:, cols],
+                start=True,
+                stop=True,
+            )
+
+        def planes(name, width=S, dtype=F32):
+            return [keep.tile([P, width], dtype, name=f"{name}{t}") for t in range(PACK)]
+
+        def banks(name):
+            return [psum.tile([P, S], F32, name=f"{name}{t}", tag="bank") for t in range(PACK)]
+
+        y = planes("y")
+        y_bank = banks("y_bank")
+        for t in range(PACK):
+            product(y_bank[t], w_words, w_scales, t, xq_words, xq_scales, slice(0, S))
+            nc.vector.tensor_copy(y[t][:], y_bank[t][:])
+        bias2 = keep.tile([P, PACK], F32, name="bias2")
+        nc.vector.scalar_tensor_tensor(bias2[:], slope2[:], -1.0, thresh2[:], ALU.mult, ALU.mult)
+
+        z_words = keep.tile([P, S], U32, name="z_words", align_bytes=64)
+        z_scales = keep.tile([P, S], U8, name="z_scales", align_bytes=64)
+        b_bank = banks("b_bank")
+        a_bank = banks("a_bank")
+        picked = {}
+
+        def pick_later(key, table, lst, dtype):
+            picked[key] = pick(table, lst, dtype, key, True)
+
+        starts = [sum(CHUNKS[:c]) for c in range(len(CHUNKS))]
+        last = len(CHUNKS) - 1
+        units = [(c, t) for c in range(len(CHUNKS)) for t in range(PACK)]
+        made = {}
+
+        def sigmoids(c, t):
+            width = CHUNKS[c]
+            sg = keep.tile([P, MEMBERS * width], F32, name=f"sg{c}_{t}")
+            for first in range(0, MEMBERS * width, PIECE):
+                nc.scalar.activation(
+                    sg[:, first : first + PIECE],
+                    y[t][:].indirect(piece(n1_l, MEMBERS * starts[c] + first)),
+                    ACT.Sigmoid,
+                    bias=bias[:, t : t + 1],
+                    scale=slope[:, t : t + 1],
+                )
+            made["sg", c, t] = sg
+
+        def add_pairs(c, t):
+            sg = made["sg", c, t]
+            pairs = keep.tile([P, 2 * CHUNKS[c]], F32, name=f"pairs{c}_{t}")
+            nc.vector.tensor_tensor(pairs[:], sg[:, 0::2], sg[:, 1::2], ALU.add)
+            made["pairs", c, t] = pairs
+
+        def count(c, t):
+            pairs = made["pairs", c, t]
+            cnt = keep.tile([P, CHUNKS[c]], F32, name=f"cnt{c}_{t}")
+            nc.vector.scalar_tensor_tensor(cnt[:], pairs[:, 0::2], -1.5, pairs[:, 1::2], ALU.add, ALU.add)
+            made["cnt", c, t] = cnt
+
+        def larger(c, t):
+            cols = slice(starts[c], starts[c] + CHUNKS[c])
+            big = keep.tile([P, CHUNKS[c]], F32, name=f"big{c}_{t}")
+            nc.vector.tensor_tensor(big[:], made["cnt", c, t][:], y[t][:, cols], ALU.max)
+            made["big", c, t] = big
+
+        z_planes = [keep.tile([P, PACK, CHUNKS[c]], BF16, name=f"z_planes{c}") for c in range(last)]
+        z_bf = [keep.tile([P, CHUNKS[c], PACK], BF16, name=f"z_bf{c}", align_bytes=64) for c in range(len(CHUNKS))]
+
+        def weigh(c, t):
+            dst = z_bf[c][:, :, t] if c == last else z_planes[c][:, t, :]
+            nc.vector.tensor_scalar(dst, made["big", c, t][:], gain[:, t : t + 1], None, ALU.mult)
+
+        def weave(c):
+            nc.vector.tensor_copy(
+                z_bf[c][:].rearrange("p (g i) t -> p g t i", i=4),
+                z_planes[c][:].rearrange("p t (g i) -> p g t i", i=4),
+            )
+
+        def quantise(c):
+            cols = slice(starts[c], starts[c] + CHUNKS[c])
+            nc.vector.quantize_mx(
+                z_words[:, cols].bitcast(FP8X4), z_scales[:, cols], z_bf[c][:].rearrange("p w t -> p (w t)")
+            )
+            for t in range(PACK):
+                product(b_bank[t], picked["xb_words"], xb_scales, t, z_words, z_scales, cols)
+            for t in range(PACK):
+                product(a_bank[t], picked["xa_words"], picked["xa_scales"], t, z_words, z_scales, cols)
+
+        fillers = {
+            0: lambda: pick_later("xb_words", table_words, cb_l, U32),
+            1: lambda: pick_later("xa_scales", table_scales, ca_l, U8),
+            2: lambda: pick_later("xa_words", table_words, ca_l, U32),
+            5: lambda: weave(0),
+            6: lambda: quantise(0),
+            7: lambda: pick_later("xd_scales", table_scales, cd_l, U8),
+            9: lambda: weave(1),
+            10: lambda: quantise(1),
+        }
+        for u, unit in enumerate(units):
+            sigmoids(*unit)
+            if u in fillers:
+                fillers[u]()
+            add_pairs(*unit)
+            if u > 0:
+                larger(*units[u - 1])
+            count(*unit)
+            if u > 0:
+                weigh(*units[u - 1])
+        larger(*units[-1])
+        weigh(*units[-1])
+
+        a_half = planes("a_half")
+        b = planes("b")
+        q = planes("q")
+        early = slice(0, starts[last])
+        late = slice(starts[last], S)
+        for t in range(PACK):
+            nc.scalar.activation(b[t][:, early], b_bank[t][:, early], ACT.Copy, scale=0.0625)
+        for t in range(PACK):
+            nc.scalar.activation(a_half[t][:, early], a_bank[t][:, early], ACT.Copy, scale=-0.03125)
+        quantise(last)
+        pick_later("xd_words", table_words, cd_l, U32)
+        for t in range(PACK):
+            nc.scalar.activation(b[t][:, late], b_bank[t][:, late], ACT.Copy, scale=0.0625)
+        for t in range(PACK):
+            nc.vector.tensor_scalar(a_half[t][:, late], a_bank[t][:, late], -0.03125, None, ALU.mult)
+        q_bank = banks("q_bank")
+        for t in range(PACK):
+            product(q_bank[t], picked["xd_words"], picked["xd_scales"], t, z_words, z_scales, slice(0, S))
+
+        sg2 = planes("sg2")
+        gated = planes("gated")
+        m1 = planes("m1")
+        q_at = planes("q_at")
+        m1_at = planes("m1_at")
+        high = planes("high")
+        low = planes("low")
+        result = planes("result")
+        halves = [slice(first, first + PIECE) for first in range(0, S, PIECE)]
+        out_rows = out.rearrange("(p t) n -> p t n", t=PACK)
+
+        def gate(t):
+            for cols in halves:
+                nc.scalar.activation(
+                    sg2[t][:, cols],
+                    b[t][:].indirect(piece(n2_l, cols.start)),
+                    ACT.Sigmoid,
+                    bias=bias2[:, t : t + 1],
+                    scale=slope2[:, t : t + 1],
+                )
+
+        def mix(t):
+            nc.vector.tensor_scalar(q[t][:], q_bank[t][:], 0.0625, None, ALU.mult)
+            for cols in halves:
+                nc.vector.scalar_tensor_tensor(
+                    gated[t][:, cols], a_half[t][:, cols], -2.0, sg2[t][:, cols], ALU.mult, ALU.mult
+                )
+            for cols in halves:
+                nc.vector.tensor_tensor(
+                    m1[t][:, cols], a_half[t][:].indirect(piece(n3_l, cols.start)), gated[t][:, cols], ALU.add
+                )
+
+        def fetch(dst, src, lst):
+            for cols in halves:
+                nc.scalar.activation(dst[:, cols], src[:].indirect(piece(lst, cols.start)), ACT.Copy)
+
+        def finish(t):
+            nc.vector.tensor_tensor(high[t][:], m1[t][:], q_at[t][:], ALU.max)
+            for cols in halves:
+                nc.vector.tensor_tensor(low[t][:, cols], m1_at[t][:, cols], q[t][:, cols], ALU.min)
+            for cols in halves:
+                nc.vector.tensor_tensor(result[t][:, cols], high[t][:, cols], low[t][:, cols], ALU.subtract)
+                nc.sync.dma_start(out_rows[:, t, cols], result[t][:, cols])
+
+        for t in range(PACK):
+            gate(t)
+            mix(t)
+            if t > 0:
+                fetch(m1_at[t - 1], m1[t - 1], n4_l)
+                finish(t - 1)
+            fetch(q_at[t], q[t], n5_l)
+        fetch(m1_at[PACK - 1], m1[PACK - 1], n4_l)
+        finish(PACK - 1)

@@ -1,6 +1,7 @@
 from contextlib import ExitStack
 
 import concourse.mybir as mybir
+from concourse.masks import make_identity
 
 F32 = mybir.dt.float32
 BF16 = mybir.dt.bfloat16
@@ -19,6 +20,10 @@ S = 512
 MEMBERS = 4
 PIECE = 256
 CHUNKS = (256, 128, 128)
+WIDE = 2 * S
+LEAD = 4
+Q_ON_VECTOR = 2
+A_ON_SCALAR = 4
 FLOPS = 4 * 2 * 512 * 512 * 512
 
 
@@ -28,7 +33,7 @@ def tile_picked_tricdgxbmaxbegc_none_p_kernel(
     nc = tc.nc
     with ExitStack() as ctx:
         keep = ctx.enter_context(tc.tile_pool(name="keep", bufs=1))
-        psum = ctx.enter_context(tc.psum_pool(name="psum", bufs=8))
+        psum = ctx.enter_context(tc.psum_pool(name="psum", bufs=1))
 
         def load_list(src, name):
             dst = keep.tile([P, src.shape[1]], U16, name=name)
@@ -40,11 +45,38 @@ def tile_picked_tricdgxbmaxbegc_none_p_kernel(
             queue.dma_start(dst[:], src.rearrange("(p t) o -> p (t o)", t=PACK))
             return dst
 
-        def piece(lst, first):
-            return lst[:, first // 16 : (first + PIECE) // 16]
+        def piece(lst, cols):
+            return lst[:, cols.start // 16 : cols.stop // 16]
+
+        def windows(name, width):
+            tiles = [keep.tile([P, width], F32, name=f"{name}{t}") for t in range(PACK)]
+            for tile in tiles:
+                nc.gpsimd.memset(tile[:, S:], 0.0)
+            return tiles
+
+        warm = keep.tile([P, 1], F32, name="warm")
+        warm_out = keep.tile([P, 1], F32, name="warm_out")
+        nc.vector.memset(warm[:], 0.0)
+        nc.scalar.activation(warm_out[:], warm[:], ACT.Sigmoid)
+        slope = load_column(sl, "slope", nc.gpsimd)
+        thresh = load_column(th, "thresh", nc.gpsimd)
+
+        def minus_product(left, right, name):
+            prod = keep.tile([P, PACK], F32, name=f"{name}_prod")
+            dst = keep.tile([P, PACK], F32, name=name)
+            nc.gpsimd.tensor_tensor(prod[:], left[:], right[:], ALU.mult)
+            nc.gpsimd.tensor_scalar(dst[:], prod[:], -1.0, 0.0, ALU.mult, ALU.add)
+            return dst
+
+        y = windows("y", WIDE)
+        bias = minus_product(slope, thresh, "bias")
+        identity = keep.tile([P, P], F32, name="identity")
+        make_identity(nc, identity[:])
 
         table_scales = keep.tile([P, T], U8, name="table_scales", align_bytes=64)
         nc.vector.memset(table_scales[:].bitcast(I32), 0)
+        offs_l = load_list(offs, "offs_l")
+        cb_l = load_list(cb, "cb_l")
         w_rows = w1.rearrange("(p j) c -> p j c", j=PACK)
         w_half = [keep.tile([P, PACK, S // 2], F32, name=f"w_half{h}") for h in range(2)]
         nc.sync.dma_start(w_half[0][:], w_rows[:, :, : S // 2])
@@ -53,18 +85,14 @@ def tile_picked_tricdgxbmaxbegc_none_p_kernel(
                 table_scales[32 * quad : 32 * quad + 4, :].bitcast(I32),
                 x_scales[0, 4 * quad : 4 * quad + 4, :].bitcast(I32),
             )
-        offs_l = load_list(offs, "offs_l")
         nc.sync.dma_start(w_half[1][:], w_rows[:, :, S // 2 :])
-        cb_l = load_list(cb, "cb_l")
         table_words = keep.tile([P, T], U32, name="table_words", align_bytes=64)
         nc.sync.dma_start(
             table_words[:].bitcast(I32), x_words[0].rearrange("p n t -> p (n t)").bitcast(I32)
         )
-        slope = load_column(sl, "slope", nc.gpsimd)
-        thresh = load_column(th, "thresh", nc.gpsimd)
         n1_l = load_list(n1, "n1_l")
-        gain = load_column(gs, "gain", nc.sync)
         ca_l = load_list(ca, "ca_l")
+        gain = load_column(gs, "gain", nc.sync)
         cd_l = load_list(cd, "cd_l")
         slope2 = load_column(sl2, "slope2", nc.sync)
         thresh2 = load_column(th2, "thresh2", nc.sync)
@@ -73,8 +101,8 @@ def tile_picked_tricdgxbmaxbegc_none_p_kernel(
         n5_l = load_list(n5, "n5_l")
         n4_l = load_list(n4, "n4_l")
 
-        def pick(table, lst, dtype, name, dealt):
-            dst = keep.tile([P, S], dtype, name=name, align_bytes=64)
+        def pick(table, lst, dtype, name, dealt, tag):
+            dst = keep.tile([P, S], dtype, name=name, tag=tag, align_bytes=64)
             view = dst[:].rearrange("p (t m) -> p m t", t=PACK) if dealt else dst[:]
             nc.vector.tensor_copy(view, table[:].indirect(lst[:]))
             return dst
@@ -86,21 +114,27 @@ def tile_picked_tricdgxbmaxbegc_none_p_kernel(
                 w_bf_view[:, h * (P // 2) : (h + 1) * (P // 2)],
                 w_half[h][:].rearrange("p j (m t) -> p m t j", t=PACK),
             )
-        xq_scales = pick(table_scales, offs_l, U8, "xq_scales", False)
-        xb_scales = pick(table_scales, cb_l, U8, "xb_scales", True)
-        w_words = keep.tile([P, S], U32, name="w_words", align_bytes=64)
-        w_scales = keep.tile([P, S], U8, name="w_scales", align_bytes=64)
-        nc.vector.quantize_mx(w_words[:].bitcast(FP8X4), w_scales[:], w_bf[:])
-        xq_words = pick(table_words, offs_l, U32, "xq_words", False)
-        bias = keep.tile([P, PACK], F32, name="bias")
-        nc.vector.scalar_tensor_tensor(bias[:], slope[:], -1.0, thresh[:], ALU.mult, ALU.mult)
+        xq_scales = pick(table_scales, offs_l, U8, "xq_scales", False, "scales_0")
+        xb_scales = pick(table_scales, cb_l, U8, "xb_scales", True, "scales_1")
+        w_words_first = keep.tile([P, P], U32, name="w_words_first", tag="words_2", align_bytes=64)
+        w_words_rest = keep.tile([P, S - P], U32, name="w_words_rest", tag="words_1", align_bytes=64)
+        w_scales = keep.tile([P, S], U8, name="w_scales", tag="scales_2", align_bytes=64)
+        nc.vector.quantize_mx(w_words_first[:].bitcast(FP8X4), w_scales[:, :P], w_bf[:, :S])
+        nc.vector.quantize_mx(w_words_rest[:].bitcast(FP8X4), w_scales[:, P:], w_bf[:, S:])
+        w_words = [w_words_first[:]] + [w_words_rest[:, t * P : (t + 1) * P] for t in range(PACK - 1)]
+        halves = [slice(first, first + PIECE) for first in range(0, S, PIECE)]
+        xq_words = keep.tile([P, S], U32, name="xq_words", tag="words_0", align_bytes=64)
+        for cols in halves:
+            nc.vector.tensor_copy(xq_words[:, cols], table_words[:].indirect(piece(offs_l, cols)))
 
-        def product(bank, words, scales, t, rhs_words, rhs_scales, cols):
-            rows = slice(t * P, (t + 1) * P)
+        def rows(t):
+            return slice(t * P, (t + 1) * P)
+
+        def product(bank, words, scales, rhs_words, rhs_scales, cols):
             nc.tensor.matmul_mx(
                 bank[:, cols],
-                lhsT=words[:, rows].bitcast(FP8X4),
-                lhsT_scale=scales[:, rows],
+                lhsT=words.bitcast(FP8X4),
+                lhsT_scale=scales,
                 rhs=rhs_words[:, cols].bitcast(FP8X4),
                 rhs_scale=rhs_scales[:, cols],
                 start=True,
@@ -110,177 +144,225 @@ def tile_picked_tricdgxbmaxbegc_none_p_kernel(
         def planes(name, width=S, dtype=F32):
             return [keep.tile([P, width], dtype, name=f"{name}{t}") for t in range(PACK)]
 
-        def banks(name):
-            return [psum.tile([P, S], F32, name=f"{name}{t}", tag="bank") for t in range(PACK)]
+        def bank_tile(name, number):
+            return psum.tile([P, S], F32, name=name, tag=f"bank{number}")
 
-        y = planes("y")
-        y_bank = banks("y_bank")
-        for t in range(PACK):
-            product(y_bank[t], w_words, w_scales, t, xq_words, xq_scales, slice(0, S))
-            nc.vector.tensor_copy(y[t][:], y_bank[t][:])
-        bias2 = keep.tile([P, PACK], F32, name="bias2")
-        nc.vector.scalar_tensor_tensor(bias2[:], slope2[:], -1.0, thresh2[:], ALU.mult, ALU.mult)
+        def banks(name, first):
+            return [bank_tile(f"{name}{t}", first + t) for t in range(PACK)]
+
+        y_parts = [(0, cols) for cols in halves] + [(t, slice(0, S)) for t in range(1, PACK)]
+        for number, (t, cols) in enumerate(y_parts):
+            y_bank = bank_tile("y_bank", PACK + 3 - number)
+            product(y_bank, w_words[t], w_scales[:, rows(t)], xq_words, xq_scales, cols)
+            nc.vector.tensor_copy(y[t][:, cols], y_bank[:, cols])
+        bias2 = minus_product(slope2, thresh2, "bias2")
 
         z_words = keep.tile([P, S], U32, name="z_words", align_bytes=64)
         z_scales = keep.tile([P, S], U8, name="z_scales", align_bytes=64)
-        b_bank = banks("b_bank")
-        a_bank = banks("a_bank")
-        picked = {}
-
-        def pick_later(key, table, lst, dtype):
-            picked[key] = pick(table, lst, dtype, key, True)
-
         starts = [sum(CHUNKS[:c]) for c in range(len(CHUNKS))]
         last = len(CHUNKS) - 1
-        units = [(c, t) for c in range(len(CHUNKS)) for t in range(PACK)]
-        made = {}
-
-        def sigmoids(c, t):
-            width = CHUNKS[c]
-            sg = keep.tile([P, MEMBERS * width], F32, name=f"sg{c}_{t}")
-            for first in range(0, MEMBERS * width, PIECE):
-                nc.scalar.activation(
-                    sg[:, first : first + PIECE],
-                    y[t][:].indirect(piece(n1_l, MEMBERS * starts[c] + first)),
-                    ACT.Sigmoid,
-                    bias=bias[:, t : t + 1],
-                    scale=slope[:, t : t + 1],
-                )
-            made["sg", c, t] = sg
-
-        def add_pairs(c, t):
-            sg = made["sg", c, t]
-            pairs = keep.tile([P, 2 * CHUNKS[c]], F32, name=f"pairs{c}_{t}")
-            nc.vector.tensor_tensor(pairs[:], sg[:, 0::2], sg[:, 1::2], ALU.add)
-            made["pairs", c, t] = pairs
-
-        def count(c, t):
-            pairs = made["pairs", c, t]
-            cnt = keep.tile([P, CHUNKS[c]], F32, name=f"cnt{c}_{t}")
-            nc.vector.scalar_tensor_tensor(cnt[:], pairs[:, 0::2], -1.5, pairs[:, 1::2], ALU.add, ALU.add)
-            made["cnt", c, t] = cnt
-
-        def larger(c, t):
-            cols = slice(starts[c], starts[c] + CHUNKS[c])
-            big = keep.tile([P, CHUNKS[c]], F32, name=f"big{c}_{t}")
-            nc.vector.tensor_tensor(big[:], made["cnt", c, t][:], y[t][:, cols], ALU.max)
-            made["big", c, t] = big
-
-        z_planes = [keep.tile([P, PACK, CHUNKS[c]], BF16, name=f"z_planes{c}") for c in range(last)]
-        z_bf = [keep.tile([P, CHUNKS[c], PACK], BF16, name=f"z_bf{c}", align_bytes=64) for c in range(len(CHUNKS))]
-
-        def weigh(c, t):
-            dst = z_bf[c][:, :, t] if c == last else z_planes[c][:, t, :]
-            nc.vector.tensor_scalar(dst, made["big", c, t][:], gain[:, t : t + 1], None, ALU.mult)
-
-        def weave(c):
-            nc.vector.tensor_copy(
-                z_bf[c][:].rearrange("p (g i) t -> p g t i", i=4),
-                z_planes[c][:].rearrange("p t (g i) -> p g t i", i=4),
-            )
-
-        def quantise(c):
-            cols = slice(starts[c], starts[c] + CHUNKS[c])
-            nc.vector.quantize_mx(
-                z_words[:, cols].bitcast(FP8X4), z_scales[:, cols], z_bf[c][:].rearrange("p w t -> p (w t)")
-            )
-            for t in range(PACK):
-                product(b_bank[t], picked["xb_words"], xb_scales, t, z_words, z_scales, cols)
-            for t in range(PACK):
-                product(a_bank[t], picked["xa_words"], picked["xa_scales"], t, z_words, z_scales, cols)
-
-        fillers = {
-            0: lambda: pick_later("xb_words", table_words, cb_l, U32),
-            1: lambda: pick_later("xa_scales", table_scales, ca_l, U8),
-            2: lambda: pick_later("xa_words", table_words, ca_l, U32),
-            5: lambda: weave(0),
-            6: lambda: quantise(0),
-            7: lambda: pick_later("xd_scales", table_scales, cd_l, U8),
-            9: lambda: weave(1),
-            10: lambda: quantise(1),
-        }
-        for u, unit in enumerate(units):
-            sigmoids(*unit)
-            if u in fillers:
-                fillers[u]()
-            add_pairs(*unit)
-            if u > 0:
-                larger(*units[u - 1])
-            count(*unit)
-            if u > 0:
-                weigh(*units[u - 1])
-        larger(*units[-1])
-        weigh(*units[-1])
-
-        a_half = planes("a_half")
-        b = planes("b")
-        q = planes("q")
         early = slice(0, starts[last])
         late = slice(starts[last], S)
+        tail = CHUNKS[last]
+        b = planes("b", WIDE)
+        a_half = planes("a_half", WIDE)
+        q = planes("q", S + 2 * tail)
+        m1 = planes("m1", WIDE)
+        big = [b[t][:, S:] for t in range(PACK)]
+        cnt = [a_half[t][:, S:] for t in range(PACK)]
+        pairs = [q[t][:, S:] for t in range(PACK)]
+        gated = [m1[t][:, S:] for t in range(PACK)]
+        sg_last = []
+        z_planes = [keep.tile([P, PACK, width], BF16, name=f"z_planes{c}") for c, width in enumerate(CHUNKS)]
+        z_bf = [keep.tile([P, width, PACK], BF16, name=f"z_bf{c}", align_bytes=64) for c, width in enumerate(CHUNKS)]
+        picked = {}
+        counts = {}
+
+        def chunk(c):
+            return slice(starts[c], starts[c] + CHUNKS[c])
+
+        def pick_later(key, table, lst, dtype, tag):
+            picked[key] = pick(table, lst, dtype, key, True, tag)
+
+        def sigmoid(t, first, slot):
+            sg = keep.tile([P, MEMBERS * P], F32, name="sg", tag=f"slot{slot}", align_bytes=64)
+            nc.scalar.activation(
+                sg[:],
+                y[t][:].indirect(piece(n1_l, slice(MEMBERS * first, MEMBERS * (first + P)))),
+                ACT.Sigmoid,
+                bias=bias[:, t : t + 1],
+                scale=slope[:, t : t + 1],
+            )
+            return sg
+
+        def early_slot(c, t, first):
+            return PACK * starts[c] // P + (t * CHUNKS[c] + first) // P
+
+        def late_slot(t):
+            return early_slot(last - 1, 1 + t % (PACK - 1), 0)
+
+        def sum_turned(c, t):
+            bank = bank_tile("turned_bank", PACK + t % 2)
+            for first in range(0, CHUNKS[c], P):
+                sg = sigmoid(t, starts[c] + first, early_slot(c, t, first))
+                for member in range(MEMBERS):
+                    nc.tensor.matmul(
+                        bank[:, first : first + P],
+                        lhsT=sg[:, member::MEMBERS],
+                        rhs=identity[:],
+                        start=member == 0,
+                        stop=member == MEMBERS - 1,
+                        is_transpose=True,
+                    )
+            counts[c, t] = bank
+
+        def turn_back(c, t):
+            cols = chunk(c)
+            nc.vector.tensor_copy(cnt[t][:, cols], counts[c, t][:, : CHUNKS[c]])
+            bank = bank_tile("count_bank", PACK + 2 + t % 2)
+            for first in range(0, CHUNKS[c], P):
+                nc.tensor.transpose(
+                    bank[:, first : first + P], cnt[t][:, cols.start + first : cols.start + first + P], identity[:]
+                )
+            counts[c, t] = bank
+
+        def larger(c, t):
+            cols = chunk(c)
+            nc.vector.scalar_tensor_tensor(
+                big[t][:, cols], counts[c, t][:, : CHUNKS[c]], -1.5, y[t][:, cols], ALU.add, ALU.max
+            )
+
+        def add_pairs(t):
+            nc.vector.tensor_tensor(pairs[t], sg_last[t][:, 0::2], sg_last[t][:, 1::2], ALU.add)
+
+        def count(t):
+            nc.vector.scalar_tensor_tensor(
+                cnt[t][:, late], pairs[t][:, 0::2], -1.5, pairs[t][:, 1::2], ALU.add, ALU.add
+            )
+
+        def larger_last(t):
+            nc.vector.tensor_tensor(big[t][:, late], cnt[t][:, late], y[t][:, late], ALU.max)
+
+        def weigh(c, t):
+            src = big[t][:, chunk(c)]
+            nc.vector.tensor_scalar(z_planes[c][:, t, :], src, gain[:, t : t + 1], None, ALU.mult)
+
+        def weave(c):
+            nc.vector.tensor_copy(z_bf[c][:], z_planes[c][:].rearrange("p t w -> p w t"))
+
+        def quantise(c):
+            nc.vector.quantize_mx(
+                z_words[:, chunk(c)].bitcast(FP8X4), z_scales[:, chunk(c)], z_bf[c][:].rearrange("p w t -> p (w t)")
+            )
+
+        def score(bank, words, scales, spans):
+            for t in range(PACK):
+                for span in spans:
+                    product(bank[t], words[:, rows(t)], scales[:, rows(t)], z_words, z_scales, span)
+
+        b_bank = banks("b_bank", 0)
+
+        def close(c, t):
+            larger(c, t)
+            weigh(c, t)
+            if t == PACK - 1:
+                weave(c)
+                quantise(c)
+                score(b_bank, picked["xb_words"], xb_scales, [chunk(c)])
+
+        fillers = [
+            lambda: pick_later("xb_words", table_words, cb_l, U32, "words_0"),
+            lambda: pick_later("xa_scales", table_scales, ca_l, U8, "scales_0"),
+            lambda: pick_later("xa_words", table_words, ca_l, U32, "slot1"),
+            lambda: pick_later("xd_scales", table_scales, cd_l, U8, "slot3"),
+            lambda: pick_later("xd_words", table_words, cd_l, U32, "slot5"),
+        ]
+        units = [(c, t) for c in range(last) for t in range(PACK)]
+        for u in range(len(units) + 1):
+            if u < len(units):
+                sum_turned(*units[u])
+            else:
+                sg_last.append(sigmoid(0, starts[last], late_slot(0)))
+            if u >= 1:
+                turn_back(*units[u - 1])
+            if u >= 2:
+                close(*units[u - 2])
+            if u < len(fillers):
+                fillers[u]()
+        for t in range(1, PACK):
+            sg_last.append(sigmoid(t, starts[last], late_slot(t)))
+        add_pairs(0)
+        close(*units[-1])
+        for t in range(PACK):
+            count(t)
+            if t > 0:
+                weigh(last, t - 1)
+            larger_last(t)
+            if t + 1 < PACK:
+                add_pairs(t + 1)
+        weigh(last, PACK - 1)
+        weave(last)
+
+        a_bank = banks("a_bank", PACK)
+        early_chunks = [chunk(c) for c in range(last)]
+        score(a_bank, picked["xa_words"], picked["xa_scales"], early_chunks)
         for t in range(PACK):
             nc.scalar.activation(b[t][:, early], b_bank[t][:, early], ACT.Copy, scale=0.0625)
-        for t in range(PACK):
+        for t in range(A_ON_SCALAR):
             nc.scalar.activation(a_half[t][:, early], a_bank[t][:, early], ACT.Copy, scale=-0.03125)
         quantise(last)
-        pick_later("xd_words", table_words, cd_l, U32)
+        score(b_bank, picked["xb_words"], xb_scales, [late])
+        score(a_bank, picked["xa_words"], picked["xa_scales"], [late])
         for t in range(PACK):
-            nc.scalar.activation(b[t][:, late], b_bank[t][:, late], ACT.Copy, scale=0.0625)
+            nc.vector.tensor_scalar(b[t][:, late], b_bank[t][:, late], 0.0625, None, ALU.mult)
+        whole = slice(0, S)
         for t in range(PACK):
-            nc.vector.tensor_scalar(a_half[t][:, late], a_bank[t][:, late], -0.03125, None, ALU.mult)
-        q_bank = banks("q_bank")
-        for t in range(PACK):
-            product(q_bank[t], picked["xd_words"], picked["xd_scales"], t, z_words, z_scales, slice(0, S))
+            rest = late if t < A_ON_SCALAR else whole
+            nc.vector.tensor_scalar(a_half[t][:, rest], a_bank[t][:, rest], -0.03125, None, ALU.mult)
+        q_bank = banks("q_bank", 0)
+        score(q_bank, picked["xd_words"], picked["xd_scales"], [slice(0, S)])
 
         sg2 = planes("sg2")
-        gated = planes("gated")
-        m1 = planes("m1")
         q_at = planes("q_at")
         m1_at = planes("m1_at")
         high = planes("high")
         low = planes("low")
         result = planes("result")
-        halves = [slice(first, first + PIECE) for first in range(0, S, PIECE)]
         out_rows = out.rearrange("(p t) n -> p t n", t=PACK)
 
         def gate(t):
-            for cols in halves:
-                nc.scalar.activation(
-                    sg2[t][:, cols],
-                    b[t][:].indirect(piece(n2_l, cols.start)),
-                    ACT.Sigmoid,
-                    bias=bias2[:, t : t + 1],
-                    scale=slope2[:, t : t + 1],
-                )
+            nc.scalar.activation(
+                sg2[t][:],
+                b[t][:].indirect(n2_l[:]),
+                ACT.Sigmoid,
+                bias=bias2[:, t : t + 1],
+                scale=slope2[:, t : t + 1],
+            )
 
         def mix(t):
-            nc.vector.tensor_scalar(q[t][:], q_bank[t][:], 0.0625, None, ALU.mult)
-            for cols in halves:
-                nc.vector.scalar_tensor_tensor(
-                    gated[t][:, cols], a_half[t][:, cols], -2.0, sg2[t][:, cols], ALU.mult, ALU.mult
-                )
-            for cols in halves:
-                nc.vector.tensor_tensor(
-                    m1[t][:, cols], a_half[t][:].indirect(piece(n3_l, cols.start)), gated[t][:, cols], ALU.add
-                )
-
-        def fetch(dst, src, lst):
-            for cols in halves:
-                nc.scalar.activation(dst[:, cols], src[:].indirect(piece(lst, cols.start)), ACT.Copy)
+            if t >= Q_ON_VECTOR:
+                nc.scalar.activation(q[t][:, whole], q_bank[t][:], ACT.Copy, scale=0.0625)
+            else:
+                nc.vector.tensor_scalar(q[t][:, whole], q_bank[t][:], 0.0625, None, ALU.mult)
+            nc.vector.scalar_tensor_tensor(gated[t], a_bank[t][:], 0.0625, sg2[t][:], ALU.mult, ALU.mult)
+            nc.vector.tensor_tensor(m1[t][:, whole], a_half[t][:].indirect(n3_l[:]), gated[t], ALU.add)
 
         def finish(t):
-            nc.vector.tensor_tensor(high[t][:], m1[t][:], q_at[t][:], ALU.max)
-            for cols in halves:
-                nc.vector.tensor_tensor(low[t][:, cols], m1_at[t][:, cols], q[t][:, cols], ALU.min)
-            for cols in halves:
-                nc.vector.tensor_tensor(result[t][:, cols], high[t][:, cols], low[t][:, cols], ALU.subtract)
+            nc.scalar.activation(q_at[t][:], q[t][:].indirect(n5_l[:]), ACT.Copy)
+            nc.vector.tensor_tensor(high[t][:], m1[t][:, whole], q_at[t][:], ALU.max)
+            spans = halves if t == PACK - 1 else [whole]
+            for cols in spans:
+                nc.scalar.activation(m1_at[t][:, cols], m1[t][:].indirect(piece(n4_l, cols)), ACT.Copy)
+                nc.vector.scalar_tensor_tensor(
+                    low[t][:, cols], q_bank[t][:, cols], 0.0625, m1_at[t][:, cols], ALU.mult, ALU.min
+                )
+                subtracts = nc.vector
+                subtracts.tensor_tensor(result[t][:, cols], high[t][:, cols], low[t][:, cols], ALU.subtract)
                 nc.sync.dma_start(out_rows[:, t, cols], result[t][:, cols])
 
-        for t in range(PACK):
-            gate(t)
-            mix(t)
-            if t > 0:
-                fetch(m1_at[t - 1], m1[t - 1], n4_l)
-                finish(t - 1)
-            fetch(q_at[t], q[t], n5_l)
-        fetch(m1_at[PACK - 1], m1[PACK - 1], n4_l)
-        finish(PACK - 1)
+        for t in range(PACK + LEAD):
+            if t >= LEAD:
+                finish(t - LEAD)
+            if t < PACK:
+                gate(t)
+                mix(t)

from contextlib import ExitStack

import concourse.mybir as mybir
from concourse.masks import make_identity

F32 = mybir.dt.float32
BF16 = mybir.dt.bfloat16
I32 = mybir.dt.int32
U32 = mybir.dt.uint32
U16 = mybir.dt.uint16
U8 = mybir.dt.uint8
FP8X4 = mybir.dt.float8_e4m3fn_x4
ALU = mybir.AluOpType
ACT = mybir.ActivationFunctionType

P = 128
PACK = 4
T = 2048
S = 512
MEMBERS = 4
PIECE = 256
CHUNKS = (256, 128, 128)
WIDE = 2 * S
LEAD = 4
Q_ON_VECTOR = 2
A_ON_SCALAR = 4
FLOPS = 4 * 2 * 512 * 512 * 512


def tile_picked_tricdgxbmaxbegc_none_p_kernel(
    tc, x_words, x_scales, w1, sl, th, gs, sl2, th2, offs, n1, ca, cb, cd, n2, n3, n4, n5, out
):
    nc = tc.nc
    with ExitStack() as ctx:
        keep = ctx.enter_context(tc.tile_pool(name="keep", bufs=1))
        psum = ctx.enter_context(tc.psum_pool(name="psum", bufs=1))

        def load_list(src, name):
            dst = keep.tile([P, src.shape[1]], U16, name=name)
            nc.sync.dma_start(dst[:], src)
            return dst

        def load_column(src, name, queue):
            dst = keep.tile([P, PACK], F32, name=name)
            queue.dma_start(dst[:], src.rearrange("(p t) o -> p (t o)", t=PACK))
            return dst

        def piece(lst, cols):
            return lst[:, cols.start // 16 : cols.stop // 16]

        def windows(name, width):
            tiles = [keep.tile([P, width], F32, name=f"{name}{t}") for t in range(PACK)]
            for tile in tiles:
                nc.gpsimd.memset(tile[:, S:], 0.0)
            return tiles

        warm = keep.tile([P, 1], F32, name="warm")
        warm_out = keep.tile([P, 1], F32, name="warm_out")
        nc.vector.memset(warm[:], 0.0)
        nc.scalar.activation(warm_out[:], warm[:], ACT.Sigmoid)
        slope = load_column(sl, "slope", nc.gpsimd)
        thresh = load_column(th, "thresh", nc.gpsimd)

        def minus_product(left, right, name):
            prod = keep.tile([P, PACK], F32, name=f"{name}_prod")
            dst = keep.tile([P, PACK], F32, name=name)
            nc.gpsimd.tensor_tensor(prod[:], left[:], right[:], ALU.mult)
            nc.gpsimd.tensor_scalar(dst[:], prod[:], -1.0, 0.0, ALU.mult, ALU.add)
            return dst

        y = windows("y", WIDE)
        bias = minus_product(slope, thresh, "bias")
        identity = keep.tile([P, P], F32, name="identity")
        make_identity(nc, identity[:])

        table_scales = keep.tile([P, T], U8, name="table_scales", align_bytes=64)
        nc.vector.memset(table_scales[:].bitcast(I32), 0)
        offs_l = load_list(offs, "offs_l")
        cb_l = load_list(cb, "cb_l")
        w_rows = w1.rearrange("(p j) c -> p j c", j=PACK)
        w_half = [keep.tile([P, PACK, S // 2], F32, name=f"w_half{h}") for h in range(2)]
        nc.sync.dma_start(w_half[0][:], w_rows[:, :, : S // 2])
        for quad in range(4):
            nc.sync.dma_start(
                table_scales[32 * quad : 32 * quad + 4, :].bitcast(I32),
                x_scales[0, 4 * quad : 4 * quad + 4, :].bitcast(I32),
            )
        nc.sync.dma_start(w_half[1][:], w_rows[:, :, S // 2 :])
        table_words = keep.tile([P, T], U32, name="table_words", align_bytes=64)
        nc.sync.dma_start(
            table_words[:].bitcast(I32), x_words[0].rearrange("p n t -> p (n t)").bitcast(I32)
        )
        n1_l = load_list(n1, "n1_l")
        ca_l = load_list(ca, "ca_l")
        gain = load_column(gs, "gain", nc.sync)
        cd_l = load_list(cd, "cd_l")
        slope2 = load_column(sl2, "slope2", nc.sync)
        thresh2 = load_column(th2, "thresh2", nc.sync)
        n2_l = load_list(n2, "n2_l")
        n3_l = load_list(n3, "n3_l")
        n5_l = load_list(n5, "n5_l")
        n4_l = load_list(n4, "n4_l")

        def pick(table, lst, dtype, name, dealt, tag):
            dst = keep.tile([P, S], dtype, name=name, tag=tag, align_bytes=64)
            view = dst[:].rearrange("p (t m) -> p m t", t=PACK) if dealt else dst[:]
            nc.vector.tensor_copy(view, table[:].indirect(lst[:]))
            return dst

        w_bf = keep.tile([P, PACK * S], BF16, name="w_bf", align_bytes=64)
        w_bf_view = w_bf[:].rearrange("p (t m j) -> p m t j", t=PACK, j=PACK)
        for h in range(2):
            nc.scalar.copy(
                w_bf_view[:, h * (P // 2) : (h + 1) * (P // 2)],
                w_half[h][:].rearrange("p j (m t) -> p m t j", t=PACK),
            )
        xq_scales = pick(table_scales, offs_l, U8, "xq_scales", False, "scales_0")
        xb_scales = pick(table_scales, cb_l, U8, "xb_scales", True, "scales_1")
        w_words_first = keep.tile([P, P], U32, name="w_words_first", tag="words_2", align_bytes=64)
        w_words_rest = keep.tile([P, S - P], U32, name="w_words_rest", tag="words_1", align_bytes=64)
        w_scales = keep.tile([P, S], U8, name="w_scales", tag="scales_2", align_bytes=64)
        nc.vector.quantize_mx(w_words_first[:].bitcast(FP8X4), w_scales[:, :P], w_bf[:, :S])
        nc.vector.quantize_mx(w_words_rest[:].bitcast(FP8X4), w_scales[:, P:], w_bf[:, S:])
        w_words = [w_words_first[:]] + [w_words_rest[:, t * P : (t + 1) * P] for t in range(PACK - 1)]
        halves = [slice(first, first + PIECE) for first in range(0, S, PIECE)]
        xq_words = keep.tile([P, S], U32, name="xq_words", tag="words_0", align_bytes=64)
        for cols in halves:
            nc.vector.tensor_copy(xq_words[:, cols], table_words[:].indirect(piece(offs_l, cols)))

        def rows(t):
            return slice(t * P, (t + 1) * P)

        def product(bank, words, scales, rhs_words, rhs_scales, cols):
            nc.tensor.matmul_mx(
                bank[:, cols],
                lhsT=words.bitcast(FP8X4),
                lhsT_scale=scales,
                rhs=rhs_words[:, cols].bitcast(FP8X4),
                rhs_scale=rhs_scales[:, cols],
                start=True,
                stop=True,
            )

        def planes(name, width=S, dtype=F32):
            return [keep.tile([P, width], dtype, name=f"{name}{t}") for t in range(PACK)]

        def bank_tile(name, number):
            return psum.tile([P, S], F32, name=name, tag=f"bank{number}")

        def banks(name, first):
            return [bank_tile(f"{name}{t}", first + t) for t in range(PACK)]

        y_parts = [(0, cols) for cols in halves] + [(t, slice(0, S)) for t in range(1, PACK)]
        for number, (t, cols) in enumerate(y_parts):
            y_bank = bank_tile("y_bank", PACK + 3 - number)
            product(y_bank, w_words[t], w_scales[:, rows(t)], xq_words, xq_scales, cols)
            nc.vector.tensor_copy(y[t][:, cols], y_bank[:, cols])
        bias2 = minus_product(slope2, thresh2, "bias2")

        z_words = keep.tile([P, S], U32, name="z_words", align_bytes=64)
        z_scales = keep.tile([P, S], U8, name="z_scales", align_bytes=64)
        starts = [sum(CHUNKS[:c]) for c in range(len(CHUNKS))]
        last = len(CHUNKS) - 1
        early = slice(0, starts[last])
        late = slice(starts[last], S)
        tail = CHUNKS[last]
        b = planes("b", WIDE)
        a_half = planes("a_half", WIDE)
        q = planes("q", S + 2 * tail)
        m1 = planes("m1", WIDE)
        big = [b[t][:, S:] for t in range(PACK)]
        cnt = [a_half[t][:, S:] for t in range(PACK)]
        pairs = [q[t][:, S:] for t in range(PACK)]
        gated = [m1[t][:, S:] for t in range(PACK)]
        sg_last = []
        z_planes = [keep.tile([P, PACK, width], BF16, name=f"z_planes{c}") for c, width in enumerate(CHUNKS)]
        z_bf = [keep.tile([P, width, PACK], BF16, name=f"z_bf{c}", align_bytes=64) for c, width in enumerate(CHUNKS)]
        picked = {}
        counts = {}

        def chunk(c):
            return slice(starts[c], starts[c] + CHUNKS[c])

        def pick_later(key, table, lst, dtype, tag):
            picked[key] = pick(table, lst, dtype, key, True, tag)

        def sigmoid(t, first, slot):
            sg = keep.tile([P, MEMBERS * P], F32, name="sg", tag=f"slot{slot}", align_bytes=64)
            nc.scalar.activation(
                sg[:],
                y[t][:].indirect(piece(n1_l, slice(MEMBERS * first, MEMBERS * (first + P)))),
                ACT.Sigmoid,
                bias=bias[:, t : t + 1],
                scale=slope[:, t : t + 1],
            )
            return sg

        def early_slot(c, t, first):
            return PACK * starts[c] // P + (t * CHUNKS[c] + first) // P

        def late_slot(t):
            return early_slot(last - 1, 1 + t % (PACK - 1), 0)

        def sum_turned(c, t):
            bank = bank_tile("turned_bank", PACK + t % 2)
            for first in range(0, CHUNKS[c], P):
                sg = sigmoid(t, starts[c] + first, early_slot(c, t, first))
                for member in range(MEMBERS):
                    nc.tensor.matmul(
                        bank[:, first : first + P],
                        lhsT=sg[:, member::MEMBERS],
                        rhs=identity[:],
                        start=member == 0,
                        stop=member == MEMBERS - 1,
                        is_transpose=True,
                    )
            counts[c, t] = bank

        def turn_back(c, t):
            cols = chunk(c)
            nc.vector.tensor_copy(cnt[t][:, cols], counts[c, t][:, : CHUNKS[c]])
            bank = bank_tile("count_bank", PACK + 2 + t % 2)
            for first in range(0, CHUNKS[c], P):
                nc.tensor.transpose(
                    bank[:, first : first + P], cnt[t][:, cols.start + first : cols.start + first + P], identity[:]
                )
            counts[c, t] = bank

        def larger(c, t):
            cols = chunk(c)
            nc.vector.scalar_tensor_tensor(
                big[t][:, cols], counts[c, t][:, : CHUNKS[c]], -1.5, y[t][:, cols], ALU.add, ALU.max
            )

        def add_pairs(t):
            nc.vector.tensor_tensor(pairs[t], sg_last[t][:, 0::2], sg_last[t][:, 1::2], ALU.add)

        def count(t):
            nc.vector.scalar_tensor_tensor(
                cnt[t][:, late], pairs[t][:, 0::2], -1.5, pairs[t][:, 1::2], ALU.add, ALU.add
            )

        def larger_last(t):
            nc.vector.tensor_tensor(big[t][:, late], cnt[t][:, late], y[t][:, late], ALU.max)

        def weigh(c, t):
            src = big[t][:, chunk(c)]
            nc.vector.tensor_scalar(z_planes[c][:, t, :], src, gain[:, t : t + 1], None, ALU.mult)

        def weave(c):
            nc.vector.tensor_copy(z_bf[c][:], z_planes[c][:].rearrange("p t w -> p w t"))

        def quantise(c):
            nc.vector.quantize_mx(
                z_words[:, chunk(c)].bitcast(FP8X4), z_scales[:, chunk(c)], z_bf[c][:].rearrange("p w t -> p (w t)")
            )

        def score(bank, words, scales, spans):
            for t in range(PACK):
                for span in spans:
                    product(bank[t], words[:, rows(t)], scales[:, rows(t)], z_words, z_scales, span)

        b_bank = banks("b_bank", 0)

        def close(c, t):
            larger(c, t)
            weigh(c, t)
            if t == PACK - 1:
                weave(c)
                quantise(c)
                score(b_bank, picked["xb_words"], xb_scales, [chunk(c)])

        fillers = [
            lambda: pick_later("xb_words", table_words, cb_l, U32, "words_0"),
            lambda: pick_later("xa_scales", table_scales, ca_l, U8, "scales_0"),
            lambda: pick_later("xa_words", table_words, ca_l, U32, "slot1"),
            lambda: pick_later("xd_scales", table_scales, cd_l, U8, "slot3"),
            lambda: pick_later("xd_words", table_words, cd_l, U32, "slot5"),
        ]
        units = [(c, t) for c in range(last) for t in range(PACK)]
        for u in range(len(units) + 1):
            if u < len(units):
                sum_turned(*units[u])
            else:
                sg_last.append(sigmoid(0, starts[last], late_slot(0)))
            if u >= 1:
                turn_back(*units[u - 1])
            if u >= 2:
                close(*units[u - 2])
            if u < len(fillers):
                fillers[u]()
        for t in range(1, PACK):
            sg_last.append(sigmoid(t, starts[last], late_slot(t)))
        add_pairs(0)
        close(*units[-1])
        for t in range(PACK):
            count(t)
            if t > 0:
                weigh(last, t - 1)
            larger_last(t)
            if t + 1 < PACK:
                add_pairs(t + 1)
        weigh(last, PACK - 1)
        weave(last)

        a_bank = banks("a_bank", PACK)
        early_chunks = [chunk(c) for c in range(last)]
        score(a_bank, picked["xa_words"], picked["xa_scales"], early_chunks)
        for t in range(PACK):
            nc.scalar.activation(b[t][:, early], b_bank[t][:, early], ACT.Copy, scale=0.0625)
        for t in range(A_ON_SCALAR):
            nc.scalar.activation(a_half[t][:, early], a_bank[t][:, early], ACT.Copy, scale=-0.03125)
        quantise(last)
        score(b_bank, picked["xb_words"], xb_scales, [late])
        score(a_bank, picked["xa_words"], picked["xa_scales"], [late])
        for t in range(PACK):
            nc.vector.tensor_scalar(b[t][:, late], b_bank[t][:, late], 0.0625, None, ALU.mult)
        whole = slice(0, S)
        for t in range(PACK):
            rest = late if t < A_ON_SCALAR else whole
            nc.vector.tensor_scalar(a_half[t][:, rest], a_bank[t][:, rest], -0.03125, None, ALU.mult)
        q_bank = banks("q_bank", 0)
        score(q_bank, picked["xd_words"], picked["xd_scales"], [slice(0, S)])

        sg2 = planes("sg2")
        q_at = planes("q_at")
        m1_at = planes("m1_at")
        high = planes("high")
        low = planes("low")
        result = planes("result")
        out_rows = out.rearrange("(p t) n -> p t n", t=PACK)

        def gate(t):
            nc.scalar.activation(
                sg2[t][:],
                b[t][:].indirect(n2_l[:]),
                ACT.Sigmoid,
                bias=bias2[:, t : t + 1],
                scale=slope2[:, t : t + 1],
            )

        def mix(t):
            if t >= Q_ON_VECTOR:
                nc.scalar.activation(q[t][:, whole], q_bank[t][:], ACT.Copy, scale=0.0625)
            else:
                nc.vector.tensor_scalar(q[t][:, whole], q_bank[t][:], 0.0625, None, ALU.mult)
            nc.vector.scalar_tensor_tensor(gated[t], a_bank[t][:], 0.0625, sg2[t][:], ALU.mult, ALU.mult)
            nc.vector.tensor_tensor(m1[t][:, whole], a_half[t][:].indirect(n3_l[:]), gated[t], ALU.add)

        def finish(t):
            nc.scalar.activation(q_at[t][:], q[t][:].indirect(n5_l[:]), ACT.Copy)
            nc.vector.tensor_tensor(high[t][:], m1[t][:, whole], q_at[t][:], ALU.max)
            spans = halves if t == PACK - 1 else [whole]
            for cols in spans:
                nc.scalar.activation(m1_at[t][:, cols], m1[t][:].indirect(piece(n4_l, cols)), ACT.Copy)
                nc.vector.scalar_tensor_tensor(
                    low[t][:, cols], q_bank[t][:, cols], 0.0625, m1_at[t][:, cols], ALU.mult, ALU.min
                )
                subtracts = nc.vector
                subtracts.tensor_tensor(result[t][:, cols], high[t][:, cols], low[t][:, cols], ALU.subtract)
                nc.sync.dma_start(out_rows[:, t, cols], result[t][:, cols])

        for t in range(PACK + LEAD):
            if t >= LEAD:
                finish(t - LEAD)
            if t < PACK:
                gate(t)
                mix(t)
